import numpy as np
import ml_dtypes


def mxq(x, axis, fmt="e4m3"):
    dtype, down = {"e4m3": (ml_dtypes.float8_e4m3fn, 7), "e5m2": (ml_dtypes.float8_e5m2, 14)}[fmt]
    v = np.moveaxis(np.asarray(x, np.float32).astype(ml_dtypes.bfloat16).astype(np.float64), axis, -1)
    blocks = v.reshape(v.shape[:-1] + (-1, 32))
    amax = np.abs(blocks).max(-1, keepdims=True)
    byte = np.maximum(np.where(amax > 0, np.frexp(amax)[1] - 1 + 127, 0) - down, 1)
    scale = np.exp2(byte - 127.0)
    codes = (blocks / scale).astype(np.float32).astype(dtype).astype(np.float64)
    return np.moveaxis((codes * scale).reshape(v.shape), -1, axis)


WIDE = False


def mx_kscale(k):
    if not WIDE:
        return np.ones(k)
    levels = np.array([10, -10, 5, -5, 0])
    if k % 512:
        return np.exp2(np.random.permutation(np.resize(levels, k // 32))).repeat(32)
    a = np.empty((k // 512, 16))
    for p in range(k // 512):
        a[p, :8] = np.random.permutation(np.resize(levels, 8))
        for g in range(8):
            far = levels[np.abs(levels - a[p, g]) >= 10]
            a[p, g + 8] = far[np.random.randint(len(far))]
    return np.exp2(a.ravel()).repeat(32)


def f64(x):
    return np.asarray(x).astype(np.float64)


def striped(idx):
    return np.tile(idx.reshape(-1, 16).T, (8, 1)).astype(np.uint16)


def unstriped(offs):
    return offs[:16].T.reshape(-1).astype(np.int64)


def pack_weight(w):
    k, n = w.shape
    w = f64(np.asarray(w, np.float32).astype(ml_dtypes.bfloat16)).reshape(k // 32, 32, n)
    amax = np.abs(w).max(1)
    byte = np.clip(np.where(amax > 0, np.frexp(amax)[1] - 1 + 127 - 7, 1), 1, 254)
    scaled = (w * np.exp2(127.0 - byte)[:, None, :]).reshape(k, n).astype(np.float32)
    words = np.ascontiguousarray(scaled.reshape(k // 512, 128, 4, n).transpose(0, 1, 3, 2)).astype(ml_dtypes.float8_e4m3fn).view(np.uint8)
    return words, np.ascontiguousarray(byte.astype(np.uint8).reshape(k // 512, 16, n))


def unpack_weight(words, scales):
    g, p, n, _ = words.shape
    vals = np.ascontiguousarray(words).view(ml_dtypes.float8_e4m3fn).astype(np.float64) * np.repeat(np.exp2(scales.astype(np.float64) - 127.0), 8, axis=1)[..., None]
    return vals.transpose(0, 1, 3, 2).reshape(g * 512, n)


def sigmoid(v):
    return 1.0 / (1.0 + np.exp(-np.maximum(v, -700.0)))


K, T, S, V = 512, 1024, 512, 512


def setup_inputs():
    n = np.random.standard_normal
    s = mx_kscale(K)[:, None]
    packed_xT = pack_weight(n((K, T)) * s)
    return {
        "x_words": packed_xT[0],
        "x_scales": packed_xT[1],
        "hT": (n((K, V)) / np.sqrt(K) / s).astype(np.float32),
        "frac": (np.random.uniform(0.3, 0.9, (V, 1))).astype(np.float32),
        "offs": striped(np.random.permutation(T)[:S]),
    }


def reference(x_words, x_scales, hT, frac, offs):
    hTq = mxq(f64(hT), 0, "e4m3")
    xq = unpack_weight(x_words, x_scales)[:, unstriped(offs)]
    y = 1.5 * (hTq.T @ xq)
    ex = np.exp(y)
    ls = np.log(ex.sum(axis=1, keepdims=True))
    lp = y - ls
    pr = np.exp(lp)
    pl = pr * lp
    negh = pl.sum(axis=1, keepdims=True)
    thr = f64(frac) * np.exp(negh)
    kp = pr * (sigmoid(2000.0 * (pr - thr)))
    tq = kp.sum(axis=1, keepdims=True)
    return 100.0 * (kp / tq)

@@ -1,0 +1,156 @@
+from contextlib import ExitStack
+
+import concourse.mybir as mybir
+
+K, T, S, V = 512, 1024, 512, 512
+FLOPS = 2 * K * V * S
+
+F32 = mybir.dt.float32
+BF16 = mybir.dt.bfloat16
+I32 = mybir.dt.int32
+U32 = mybir.dt.uint32
+U16 = mybir.dt.uint16
+U8 = mybir.dt.uint8
+FP8X4 = mybir.dt.float8_e4m3fn_x4
+ALU = mybir.AluOpType
+ACT = mybir.ActivationFunctionType
+
+P = 128
+PACK = 4
+TILES = V // P
+
+
+def tile_picked_ytyp_eta_p_kernel(tc, x_words, x_scales, hT, frac, offs, out):
+    nc = tc.nc
+    with ExitStack() as ctx:
+        keep = ctx.enter_context(tc.tile_pool(name="keep", bufs=1))
+        psum = ctx.enter_context(tc.psum_pool(name="psum", bufs=1))
+
+        offsets = keep.tile([P, S // 16], U16, name="offsets")
+        words = keep.tile([P, T], U32, name="words", align_bytes=64)
+        bytes_in = keep.tile([P, T], U8, name="bytes_in", align_bytes=64)
+        x_codes = keep.tile([P, S], U32, name="x_codes", align_bytes=64)
+        x_plane = keep.tile([P, S], U8, name="x_plane", align_bytes=64)
+
+        def load_hidden(first, count):
+            raw = keep.tile([P, PACK, count * P], F32, name="h_raw%d" % first)
+            cols = slice(first * P, (first + count) * P)
+            nc.sync.dma_start(raw[:], hT[:, cols].rearrange("(p j) w -> p j w", j=PACK))
+            return [raw[:, :, c * P : (c + 1) * P] for c in range(count)]
+
+        nc.vector.memset(bytes_in[:].bitcast(I32), 0)
+        nc.sync.dma_start(offsets[:], offs)
+        h_raw = load_hidden(0, 1)
+        for q in range(4):
+            queue = nc.sync if q < 2 else nc.scalar
+            queue.dma_start(
+                bytes_in[32 * q : 32 * q + 4, :].bitcast(I32), x_scales[0, 4 * q : 4 * q + 4, :].bitcast(I32)
+            )
+        nc.sync.dma_start(words[:].bitcast(I32), x_words[0].rearrange("p n t -> p (n t)").bitcast(I32))
+        h_raw = h_raw + load_hidden(1, 1) + load_hidden(2, 2)
+        share = keep.tile([P, TILES, 1], F32, name="share")
+        with nc.allow_non_contiguous_dma(reason="one value a row"):
+            nc.sync.dma_start(share[:], frac.rearrange("(i p) o -> p i o", p=P))
+
+        nc.vector.tensor_copy(x_plane[:], bytes_in[:].indirect(offsets[:]))
+        half = S // 2
+        for c in range(2):
+            nc.vector.tensor_copy(
+                x_codes[:, c * half : (c + 1) * half], words[:].indirect(offsets[:, c * 16 : (c + 1) * 16])
+            )
+
+        factors = keep.tile([P, TILES, 2], F32, name="factors")
+        nc.gpsimd.memset(factors[:], 1000.0)
+        nc.gpsimd.tensor_scalar(factors[:, :, 1:2], share[:], -1000.0, 0.0, ALU.mult, ALU.add)
+
+        def col(name, i, width=1):
+            return keep.tile([P, width], F32, name="%s%d" % (name, i))
+
+        def wide(name, i):
+            return keep.tile([P, S], F32, name="%s%d" % (name, i))
+
+        acc = {}
+        neg_max = {}
+        ex = {}
+        total = {}
+        th = {}
+
+        def product(i):
+            grouped = keep.tile([P, P, PACK], BF16, name="grouped%d" % i, align_bytes=64)
+            nc.scalar.activation(grouped[:], h_raw[i].rearrange("p j w -> p w j"), ACT.Copy)
+            h_codes = keep.tile([P, P], U32, name="h_codes%d" % i, align_bytes=64)
+            h_plane = keep.tile([P, P], U8, name="h_plane%d" % i, align_bytes=64)
+            nc.vector.quantize_mx(
+                out=h_codes[:].bitcast(FP8X4), scales=h_plane[:], in_=grouped[:].rearrange("p w j -> p (w j)")
+            )
+            acc[i] = psum.tile([P, S], F32, name="acc%d" % i)
+            width = half if i == 0 else S
+            for c in range(0, S, width):
+                nc.tensor.matmul_mx(
+                    out=acc[i][:, c : c + width],
+                    lhsT=h_codes[:].bitcast(FP8X4),
+                    lhsT_scale=h_plane[:],
+                    rhs=x_codes[:, c : c + width].bitcast(FP8X4),
+                    rhs_scale=x_plane[:, c : c + width],
+                    start=True,
+                    stop=True,
+                )
+
+        def softmax_head(i):
+            neg_y = wide("neg_y", i)
+            neg_max[i] = col("neg_max", i)
+            nc.vector.tensor_scalar(neg_y[:], acc[i][:], -1.5, None, ALU.mult, ALU.min, accum_out=neg_max[i][:])
+            ex[i] = wide("ex", i)
+            total[i] = col("total", i)
+            nc.scalar.activation(
+                ex[i][:], neg_y[:], ACT.Exp, bias=neg_max[i][:], scale=-1.0, accum_out=total[i][:]
+            )
+
+        def gate(i):
+            inv_total = col("inv_total", i)
+            nc.vector.reciprocal(inv_total[:], total[i][:])
+            weighted = wide("weighted", i)
+            moment = col("moment", i)
+            nc.vector.scalar_tensor_tensor(
+                weighted[:], acc[i][:], 1.5, ex[i][:], ALU.mult, ALU.mult, accum_out=moment[:]
+            )
+            coef = col("coef", i, 2)
+            nc.gpsimd.tensor_scalar(coef[:], factors[:, i, :], inv_total[:], 0.0, ALU.mult, ALU.add)
+            level = col("level", i)
+            nc.scalar.activation(level[:], moment[:], ACT.Exp, bias=neg_max[i][:], scale=inv_total[:])
+            shift = col("shift", i)
+            nc.scalar.activation(shift[:], level[:], ACT.Copy, scale=coef[:, 1:2])
+            th[i] = wide("th", i)
+            nc.scalar.activation(th[i][:], ex[i][:], ACT.Tanh, bias=shift[:], scale=coef[:, 0:1])
+
+        def finish(i):
+            kept = wide("kept", i)
+            kept_sum = col("kept_sum", i)
+            nc.vector.scalar_tensor_tensor(
+                kept[:], th[i][:], 1.0, ex[i][:], ALU.add, ALU.mult, accum_out=kept_sum[:]
+            )
+            inv_kept = col("inv_kept", i)
+            nc.vector.reciprocal(inv_kept[:], kept_sum[:])
+            result = wide("result", i)
+            if i == TILES - 1:
+                nc.vector.tensor_scalar(result[:], kept[:], inv_kept[:], 100.0, ALU.mult, ALU.mult)
+            else:
+                percent = col("percent", i)
+                nc.scalar.activation(percent[:], inv_kept[:], ACT.Copy, scale=100.0)
+                nc.scalar.activation(result[:], kept[:], ACT.Copy, scale=percent[:])
+            nc.sync.dma_start(out[i * P : (i + 1) * P, :], result[:])
+
+        for i in range(TILES):
+            product(i)
+        softmax_head(0)
+        softmax_head(1)
+        gate(0)
+        softmax_head(2)
+        gate(1)
+        softmax_head(3)
+        gate(2)
+        finish(0)
+        gate(3)
+        finish(1)
+        finish(2)
+        finish(3)

@@ -33,7 +33,7 @@ def tile_picked_ytyp_eta_p_kernel(tc, x_words, x_scales, hT, frac, offs, out):
         x_plane = keep.tile([P, S], U8, name="x_plane", align_bytes=64)
 
         def load_hidden(first, count):
-            raw = keep.tile([P, PACK, count * P], F32, name="h_raw%d" % first)
+            raw = keep.tile([P, PACK, count * P], F32, name="h_raw%d" % first, tag="raw%d" % first)
             cols = slice(first * P, (first + count) * P)
             nc.sync.dma_start(raw[:], hT[:, cols].rearrange("(p j) w -> p j w", j=PACK))
             return [raw[:, :, c * P : (c + 1) * P] for c in range(count)]
@@ -47,7 +47,7 @@ def tile_picked_ytyp_eta_p_kernel(tc, x_words, x_scales, hT, frac, offs, out):
                 bytes_in[32 * q : 32 * q + 4, :].bitcast(I32), x_scales[0, 4 * q : 4 * q + 4, :].bitcast(I32)
             )
         nc.sync.dma_start(words[:].bitcast(I32), x_words[0].rearrange("p n t -> p (n t)").bitcast(I32))
-        h_raw = h_raw + load_hidden(1, 1) + load_hidden(2, 2)
+        h_raw = h_raw + load_hidden(1, 1) + load_hidden(2, 1) + load_hidden(3, 1)
         share = keep.tile([P, TILES, 1], F32, name="share")
         with nc.allow_non_contiguous_dma(reason="one value a row"):
             nc.sync.dma_start(share[:], frac.rearrange("(i p) o -> p i o", p=P))
@@ -66,8 +66,13 @@ def tile_picked_ytyp_eta_p_kernel(tc, x_words, x_scales, hT, frac, offs, out):
         def col(name, i, width=1):
             return keep.tile([P, width], F32, name="%s%d" % (name, i))
 
+        reuse = {"neg_y0": "raw2", "ex0": "raw3"}
+
         def wide(name, i):
-            return keep.tile([P, S], F32, name="%s%d" % (name, i))
+            full = "%s%d" % (name, i)
+            if full == "neg_y2":
+                return keep.tile([P, S], F32, name=full, tag="grouped3", align_bytes=64)
+            return keep.tile([P, S], F32, name=full, tag=reuse.get(full, full))
 
         acc = {}
         neg_max = {}
@@ -76,8 +81,12 @@ def tile_picked_ytyp_eta_p_kernel(tc, x_words, x_scales, hT, frac, offs, out):
         th = {}
 
         def product(i):
-            grouped = keep.tile([P, P, PACK], BF16, name="grouped%d" % i, align_bytes=64)
-            nc.scalar.activation(grouped[:], h_raw[i].rearrange("p j w -> p w j"), ACT.Copy)
+            grouped = keep.tile([P, P, PACK], BF16, name="grouped%d" % i, tag="grouped%d" % i, align_bytes=64)
+            nc.scalar.activation(
+                grouped[:].rearrange("p (c i) j -> p c j i", i=4),
+                h_raw[i].rearrange("p j (c i) -> p c j i", i=4),
+                ACT.Copy,
+            )
             h_codes = keep.tile([P, P], U32, name="h_codes%d" % i, align_bytes=64)
             h_plane = keep.tile([P, P], U8, name="h_plane%d" % i, align_bytes=64)
             nc.vector.quantize_mx(
@@ -130,27 +139,17 @@ def tile_picked_ytyp_eta_p_kernel(tc, x_words, x_scales, hT, frac, offs, out):
                 kept[:], th[i][:], 1.0, ex[i][:], ALU.add, ALU.mult, accum_out=kept_sum[:]
             )
             inv_kept = col("inv_kept", i)
-            nc.vector.reciprocal(inv_kept[:], kept_sum[:])
             result = wide("result", i)
-            if i == TILES - 1:
-                nc.vector.tensor_scalar(result[:], kept[:], inv_kept[:], 100.0, ALU.mult, ALU.mult)
-            else:
-                percent = col("percent", i)
-                nc.scalar.activation(percent[:], inv_kept[:], ACT.Copy, scale=100.0)
-                nc.scalar.activation(result[:], kept[:], ACT.Copy, scale=percent[:])
+            nc.vector.reciprocal(inv_kept[:], kept_sum[:])
+            nc.vector.tensor_scalar(result[:], kept[:], inv_kept[:], 100.0, ALU.mult, ALU.mult)
             nc.sync.dma_start(out[i * P : (i + 1) * P, :], result[:])
 
         for i in range(TILES):
             product(i)
-        softmax_head(0)
-        softmax_head(1)
-        gate(0)
-        softmax_head(2)
-        gate(1)
-        softmax_head(3)
-        gate(2)
-        finish(0)
-        gate(3)
-        finish(1)
-        finish(2)
-        finish(3)
+        for step in range(TILES + 3):
+            if step < TILES:
+                softmax_head(step)
+            if 0 <= step - 1 < TILES:
+                gate(step - 1)
+            if 0 <= step - 3 < TILES:
+                finish(step - 3)

from contextlib import ExitStack

import concourse.mybir as mybir

K, T, S, V = 512, 1024, 512, 512
FLOPS = 2 * K * V * S

F32 = mybir.dt.float32
BF16 = mybir.dt.bfloat16
I32 = mybir.dt.int32
U32 = mybir.dt.uint32
U16 = mybir.dt.uint16
U8 = mybir.dt.uint8
FP8X4 = mybir.dt.float8_e4m3fn_x4
ALU = mybir.AluOpType
ACT = mybir.ActivationFunctionType

P = 128
PACK = 4
TILES = V // P


def tile_picked_ytyp_eta_p_kernel(tc, x_words, x_scales, hT, frac, offs, out):
    nc = tc.nc
    with ExitStack() as ctx:
        keep = ctx.enter_context(tc.tile_pool(name="keep", bufs=1))
        psum = ctx.enter_context(tc.psum_pool(name="psum", bufs=1))

        offsets = keep.tile([P, S // 16], U16, name="offsets")
        words = keep.tile([P, T], U32, name="words", align_bytes=64)
        bytes_in = keep.tile([P, T], U8, name="bytes_in", align_bytes=64)
        x_codes = keep.tile([P, S], U32, name="x_codes", align_bytes=64)
        x_plane = keep.tile([P, S], U8, name="x_plane", align_bytes=64)

        def load_hidden(first, count):
            raw = keep.tile([P, PACK, count * P], F32, name="h_raw%d" % first, tag="raw%d" % first)
            cols = slice(first * P, (first + count) * P)
            nc.sync.dma_start(raw[:], hT[:, cols].rearrange("(p j) w -> p j w", j=PACK))
            return [raw[:, :, c * P : (c + 1) * P] for c in range(count)]

        nc.vector.memset(bytes_in[:].bitcast(I32), 0)
        nc.sync.dma_start(offsets[:], offs)
        h_raw = load_hidden(0, 1)
        for q in range(4):
            queue = nc.sync if q < 2 else nc.scalar
            queue.dma_start(
                bytes_in[32 * q : 32 * q + 4, :].bitcast(I32), x_scales[0, 4 * q : 4 * q + 4, :].bitcast(I32)
            )
        nc.sync.dma_start(words[:].bitcast(I32), x_words[0].rearrange("p n t -> p (n t)").bitcast(I32))
        h_raw = h_raw + load_hidden(1, 1) + load_hidden(2, 1) + load_hidden(3, 1)
        share = keep.tile([P, TILES, 1], F32, name="share")
        with nc.allow_non_contiguous_dma(reason="one value a row"):
            nc.sync.dma_start(share[:], frac.rearrange("(i p) o -> p i o", p=P))

        nc.vector.tensor_copy(x_plane[:], bytes_in[:].indirect(offsets[:]))
        half = S // 2
        for c in range(2):
            nc.vector.tensor_copy(
                x_codes[:, c * half : (c + 1) * half], words[:].indirect(offsets[:, c * 16 : (c + 1) * 16])
            )

        factors = keep.tile([P, TILES, 2], F32, name="factors")
        nc.gpsimd.memset(factors[:], 1000.0)
        nc.gpsimd.tensor_scalar(factors[:, :, 1:2], share[:], -1000.0, 0.0, ALU.mult, ALU.add)

        def col(name, i, width=1):
            return keep.tile([P, width], F32, name="%s%d" % (name, i))

        reuse = {"neg_y0": "raw2", "ex0": "raw3"}

        def wide(name, i):
            full = "%s%d" % (name, i)
            if full == "neg_y2":
                return keep.tile([P, S], F32, name=full, tag="grouped3", align_bytes=64)
            return keep.tile([P, S], F32, name=full, tag=reuse.get(full, full))

        acc = {}
        neg_max = {}
        ex = {}
        total = {}
        th = {}

        def product(i):
            grouped = keep.tile([P, P, PACK], BF16, name="grouped%d" % i, tag="grouped%d" % i, align_bytes=64)
            nc.scalar.activation(
                grouped[:].rearrange("p (c i) j -> p c j i", i=4),
                h_raw[i].rearrange("p j (c i) -> p c j i", i=4),
                ACT.Copy,
            )
            h_codes = keep.tile([P, P], U32, name="h_codes%d" % i, align_bytes=64)
            h_plane = keep.tile([P, P], U8, name="h_plane%d" % i, align_bytes=64)
            nc.vector.quantize_mx(
                out=h_codes[:].bitcast(FP8X4), scales=h_plane[:], in_=grouped[:].rearrange("p w j -> p (w j)")
            )
            acc[i] = psum.tile([P, S], F32, name="acc%d" % i)
            width = half if i == 0 else S
            for c in range(0, S, width):
                nc.tensor.matmul_mx(
                    out=acc[i][:, c : c + width],
                    lhsT=h_codes[:].bitcast(FP8X4),
                    lhsT_scale=h_plane[:],
                    rhs=x_codes[:, c : c + width].bitcast(FP8X4),
                    rhs_scale=x_plane[:, c : c + width],
                    start=True,
                    stop=True,
                )

        def softmax_head(i):
            neg_y = wide("neg_y", i)
            neg_max[i] = col("neg_max", i)
            nc.vector.tensor_scalar(neg_y[:], acc[i][:], -1.5, None, ALU.mult, ALU.min, accum_out=neg_max[i][:])
            ex[i] = wide("ex", i)
            total[i] = col("total", i)
            nc.scalar.activation(
                ex[i][:], neg_y[:], ACT.Exp, bias=neg_max[i][:], scale=-1.0, accum_out=total[i][:]
            )

        def gate(i):
            inv_total = col("inv_total", i)
            nc.vector.reciprocal(inv_total[:], total[i][:])
            weighted = wide("weighted", i)
            moment = col("moment", i)
            nc.vector.scalar_tensor_tensor(
                weighted[:], acc[i][:], 1.5, ex[i][:], ALU.mult, ALU.mult, accum_out=moment[:]
            )
            coef = col("coef", i, 2)
            nc.gpsimd.tensor_scalar(coef[:], factors[:, i, :], inv_total[:], 0.0, ALU.mult, ALU.add)
            level = col("level", i)
            nc.scalar.activation(level[:], moment[:], ACT.Exp, bias=neg_max[i][:], scale=inv_total[:])
            shift = col("shift", i)
            nc.scalar.activation(shift[:], level[:], ACT.Copy, scale=coef[:, 1:2])
            th[i] = wide("th", i)
            nc.scalar.activation(th[i][:], ex[i][:], ACT.Tanh, bias=shift[:], scale=coef[:, 0:1])

        def finish(i):
            kept = wide("kept", i)
            kept_sum = col("kept_sum", i)
            nc.vector.scalar_tensor_tensor(
                kept[:], th[i][:], 1.0, ex[i][:], ALU.add, ALU.mult, accum_out=kept_sum[:]
            )
            inv_kept = col("inv_kept", i)
            result = wide("result", i)
            nc.vector.reciprocal(inv_kept[:], kept_sum[:])
            nc.vector.tensor_scalar(result[:], kept[:], inv_kept[:], 100.0, ALU.mult, ALU.mult)
            nc.sync.dma_start(out[i * P : (i + 1) * P, :], result[:])

        for i in range(TILES):
            product(i)
        for step in range(TILES + 3):
            if step < TILES:
                softmax_head(step)
            if 0 <= step - 1 < TILES:
                gate(step - 1)
            if 0 <= step - 3 < TILES:
                finish(step - 3)
